import numpy as np
import ml_dtypes


def mxq(x, axis, fmt="e4m3"):
    dtype, down = {"e4m3": (ml_dtypes.float8_e4m3fn, 7), "e5m2": (ml_dtypes.float8_e5m2, 14)}[fmt]
    v = np.moveaxis(np.asarray(x, np.float32).astype(ml_dtypes.bfloat16).astype(np.float64), axis, -1)
    blocks = v.reshape(v.shape[:-1] + (-1, 32))
    amax = np.abs(blocks).max(-1, keepdims=True)
    byte = np.maximum(np.where(amax > 0, np.frexp(amax)[1] - 1 + 127, 0) - down, 1)
    scale = np.exp2(byte - 127.0)
    codes = (blocks / scale).astype(np.float32).astype(dtype).astype(np.float64)
    return np.moveaxis((codes * scale).reshape(v.shape), -1, axis)


WIDE = False


def mx_kscale(k):
    if not WIDE:
        return np.ones(k)
    levels = np.array([10, -10, 5, -5, 0])
    if k % 512:
        return np.exp2(np.random.permutation(np.resize(levels, k // 32))).repeat(32)
    a = np.empty((k // 512, 16))
    for p in range(k // 512):
        a[p, :8] = np.random.permutation(np.resize(levels, 8))
        for g in range(8):
            far = levels[np.abs(levels - a[p, g]) >= 10]
            a[p, g + 8] = far[np.random.randint(len(far))]
    return np.exp2(a.ravel()).repeat(32)


def f64(x):
    return np.asarray(x).astype(np.float64)


def striped(idx):
    return np.tile(idx.reshape(-1, 16).T, (8, 1)).astype(np.uint16)


def unstriped(offs):
    return offs[:16].T.reshape(-1).astype(np.int64)


def pack_weight(w):
    k, n = w.shape
    w = f64(np.asarray(w, np.float32).astype(ml_dtypes.bfloat16)).reshape(k // 32, 32, n)
    amax = np.abs(w).max(1)
    byte = np.clip(np.where(amax > 0, np.frexp(amax)[1] - 1 + 127 - 7, 1), 1, 254)
    scaled = (w * np.exp2(127.0 - byte)[:, None, :]).reshape(k, n).astype(np.float32)
    words = np.ascontiguousarray(scaled.reshape(k // 512, 128, 4, n).transpose(0, 1, 3, 2)).astype(ml_dtypes.float8_e4m3fn).view(np.uint8)
    return words, np.ascontiguousarray(byte.astype(np.uint8).reshape(k // 512, 16, n))


def unpack_weight(words, scales):
    g, p, n, _ = words.shape
    vals = np.ascontiguousarray(words).view(ml_dtypes.float8_e4m3fn).astype(np.float64) * np.repeat(np.exp2(scales.astype(np.float64) - 127.0), 8, axis=1)[..., None]
    return vals.transpose(0, 1, 3, 2).reshape(g * 512, n)


E2M1 = np.array([0.0, 0.5, 1.0, 1.5, 2.0, 3.0, 4.0, 6.0, -0.0, -0.5, -1.0, -1.5, -2.0, -3.0, -4.0, -6.0])


def pack_fp4(w):
    k, n = w.shape
    w = f64(np.asarray(w, np.float32).astype(ml_dtypes.bfloat16)).reshape(k // 32, 32, n)
    amax = np.abs(w).max(1)
    mant, ex = np.frexp(amax / 6.0)
    byte = np.clip(np.where(amax > 0, np.where(mant > 0.5, ex, ex - 1) + 127, 1), 1, 254)
    scaled = (w * np.exp2(127.0 - byte)[:, None, :]).reshape(k, n).astype(np.float32)
    c = np.ascontiguousarray(scaled.reshape(k // 512, 128, 4, n).transpose(0, 1, 3, 2)).astype(ml_dtypes.float4_e2m1fn).view(np.uint8) & 0xF
    words = (c[..., 0::2] | (c[..., 1::2] << 4)).reshape(k // 512, 128, 2 * n)
    return np.ascontiguousarray(words), np.ascontiguousarray(byte.astype(np.uint8).reshape(k // 512, 16, n))


def unpack_fp4(words, scales):
    g, _, n = scales.shape
    words = np.ascontiguousarray(words).reshape(g, 128, n, 2)
    nib = np.empty((g, 128, n, 4), np.uint8)
    nib[..., 0::2] = words & 0xF
    nib[..., 1::2] = words >> 4
    vals = E2M1[nib] * np.repeat(np.exp2(scales.astype(np.float64) - 127.0), 8, axis=1)[..., None]
    return vals.transpose(0, 1, 3, 2).reshape(g * 512, n)


def sigmoid(v):
    return 1.0 / (1.0 + np.exp(-np.maximum(v, -700.0)))


K, T, S, N, H = 512, 2048, 512, 256, 512


def setup_inputs():
    n = np.random.standard_normal
    s = mx_kscale(K)[:, None]
    u = mx_kscale(H)
    packed_xT = pack_weight(n((K, T)) * s)
    packed_w1 = pack_fp4(n((K, H)) / np.sqrt(K) / s)
    packed_w2 = pack_fp4(n((K, H)) / np.sqrt(K) / s)
    packed_w3 = pack_fp4(n((H, N)) / np.sqrt(H) / u[:, None])
    return {
        "x_words": packed_xT[0],
        "x_scales": packed_xT[1],
        "w1_words": packed_w1[0],
        "w1_scales": packed_w1[1],
        "w2_words": packed_w2[0],
        "w2_scales": packed_w2[1],
        "unit": (np.random.uniform(0.6, 1.4, (H, 1)) * u[:, None]).astype(np.float32),
        "w3_words": packed_w3[0],
        "w3_scales": packed_w3[1],
        "offs": striped(np.random.permutation(T)[:S]),
        "wrp": striped(np.random.permutation(S)),
        "wr2": striped(np.random.permutation(S)),
    }


def reference(x_words, x_scales, w1_words, w1_scales, w2_words, w2_scales, unit, w3_words, w3_scales, offs, wrp, wr2):
    xq = unpack_weight(x_words, x_scales)[:, unstriped(offs)]
    fu = unpack_fp4(w1_words, w1_scales).T @ xq
    fw = np.tanh(fu)
    bu = unpack_fp4(w2_words, w2_scales).T @ xq
    bv = np.tanh(bu)
    bw = bv[:, unstriped(wrp)]
    inc = fw + bw
    occ = sigmoid(4.0 * ((inc) ** 2 - (0.3 * ((fw) ** 2 + (bw) ** 2)) - 0.2))
    f2 = fw[:, unstriped(wr2)]
    comp = f2 - fw
    fix = (-1.0 * occ + 1.0) * fw + occ * comp
    hid = f64(unit) * (fix * occ[:, unstriped(wr2)])
    return unpack_fp4(w3_words, w3_scales).T @ mxq(hid, 0, "e4m3")

@@ -1,0 +1,217 @@
+import math
+from contextlib import ExitStack
+
+import concourse.mybir as mybir
+
+K, T, S, H, N = 512, 2048, 512, 512, 256
+FLOPS = 2 * K * H * S * 2 + 2 * H * N * S
+
+F32 = mybir.dt.float32
+BF16 = mybir.dt.bfloat16
+I32 = mybir.dt.int32
+U32 = mybir.dt.uint32
+U16 = mybir.dt.uint16
+U8 = mybir.dt.uint8
+FP8X4 = mybir.dt.float8_e4m3fn_x4
+FP4X4 = mybir.dt.float4_e2m1fn_x4
+ALU = mybir.AluOpType
+ACT = mybir.ActivationFunctionType
+
+P = 128
+PACK = 4
+HALF = S // 2
+HALVES = [slice(0, HALF), slice(HALF, S)]
+CHUNKS = [slice(0, 256), slice(256, 384), slice(384, 512)]
+EARLY = 3
+ROOT_SUM = 8.0 / 2.8
+ROOT_A = ROOT_SUM / 2 + math.sqrt(ROOT_SUM * ROOT_SUM / 4 - 1)
+ROOT_B = ROOT_SUM / 2 - math.sqrt(ROOT_SUM * ROOT_SUM / 4 - 1)
+
+
+def entries(offsets, cols):
+    return offsets[:, cols.start // 16 : cols.stop // 16]
+
+
+def load_scale_rows(queues, plane, scales):
+    for q, queue in enumerate(queues):
+        queue.dma_start(out=plane[32 * q : 32 * q + 4, :].bitcast(I32), in_=scales[0, 4 * q : 4 * q + 4, :].bitcast(I32))
+
+
+def gather(nc, on_vector, out, window, offsets):
+    if on_vector:
+        nc.vector.tensor_copy(out, window[:].indirect(offsets))
+    else:
+        nc.scalar.activation(out, window[:].indirect(offsets), ACT.Copy)
+
+
+def tile_picked_yfbflo_occ_p_kernel(
+    tc, x_words, x_scales, w1_words, w1_scales, w2_words, w2_scales, unit, w3_words, w3_scales, offs, wrp, wr2, out
+):
+    nc = tc.nc
+    with ExitStack() as ctx:
+        held = ctx.enter_context(tc.tile_pool(name="held", bufs=1))
+        psum = ctx.enter_context(tc.psum_pool(name="psum", bufs=8))
+
+        offs_t = held.tile([P, S // 16], U16, name="offs_t")
+        wrp_t = held.tile([P, S // 16], U16, name="wrp_t")
+        wr2_t = held.tile([P, S // 16], U16, name="wr2_t")
+        x_codes = held.tile([P, T], U32, name="x_codes")
+        x_plane = held.tile([P, T], U8, name="x_plane")
+        raw_codes = [held.tile([P, 2 * H], U8, name=f"raw_codes{w}", tag=f"raw{w}", align_bytes=64) for w in range(2)]
+        raw_plane = [held.tile([P, H], U8, name=f"raw_plane{w}") for w in range(2)]
+        w3_plane = held.tile([P, N], U8, name="w3_plane", align_bytes=64)
+
+        nc.vector.memset(x_plane[:].bitcast(I32), 0)
+        for plane in raw_plane + [w3_plane]:
+            nc.gpsimd.memset(plane[:].bitcast(I32), 0)
+
+        nc.sync.dma_start(offs_t[:], offs)
+        nc.scalar.dma_start(out=raw_codes[0][:].bitcast(I32), in_=w2_words[0].bitcast(I32))
+        nc.sync.dma_start(wrp_t[:], wrp)
+        nc.scalar.dma_start(out=raw_codes[1][:].bitcast(I32), in_=w1_words[0].bitcast(I32))
+        nc.sync.dma_start(wr2_t[:], wr2)
+        nc.scalar.dma_start(out=x_codes[:].bitcast(I32), in_=x_words[0].rearrange("p n t -> p (n t)").bitcast(I32))
+        load_scale_rows([nc.sync] * 4, x_plane, x_scales)
+        load_scale_rows([nc.sync] * 3 + [nc.gpsimd], raw_plane[0], w2_scales)
+        load_scale_rows([nc.sync] * 4, raw_plane[1], w1_scales)
+        load_scale_rows([nc.sync] * 4, w3_plane, w3_scales)
+
+        w_codes = [held.tile([P, PACK, 2 * P], U8, name=f"w_codes{w}", align_bytes=64) for w in range(2)]
+        w_plane = [held.tile([P, PACK, P], U8, name=f"w_plane{w}", align_bytes=64) for w in range(2)]
+        for w in range(2):
+            nc.vector.tensor_copy(
+                w_codes[w][:].rearrange("p t (m b) -> p t m b", b=2),
+                raw_codes[w][:].rearrange("p (m t b) -> p t m b", t=PACK, b=2),
+            )
+        unit_t = held.tile([P, PACK], F32, name="unit_t", tag="raw0", align_bytes=64)
+        w3_codes = held.tile([P, 2 * N], U8, name="w3_codes", tag="raw1", align_bytes=64)
+        nc.sync.dma_start(out=unit_t[:], in_=unit.rearrange("(p t) o -> p (t o)", t=PACK))
+        nc.sync.dma_start(out=w3_codes[:].bitcast(I32), in_=w3_words[0].bitcast(I32))
+        xg_codes = [held.tile([P, HALF], U32, name=f"xg_codes{h}", align_bytes=64) for h in range(2)]
+        xg_plane = [held.tile([P, HALF], U8, name=f"xg_plane{h}", align_bytes=64) for h in range(2)]
+
+        def deal_plane(w):
+            nc.vector.tensor_copy(w_plane[w][:], raw_plane[w][:].rearrange("p (m t) -> p t m", t=PACK))
+
+        nc.vector.tensor_copy(xg_plane[0][:], x_plane[:].indirect(entries(offs_t, HALVES[0])))
+        deal_plane(0)
+        nc.vector.tensor_copy(xg_codes[0][:], x_codes[:].indirect(entries(offs_t, HALVES[0])))
+        nc.vector.tensor_copy(xg_plane[1][:], x_plane[:].indirect(entries(offs_t, HALVES[1])))
+        nc.vector.tensor_copy(xg_codes[1][:], x_codes[:].indirect(entries(offs_t, HALVES[1])))
+        deal_plane(1)
+
+        def row_tiles(name):
+            return [held.tile([P, S], F32, name=f"{name}{t}") for t in range(PACK)]
+
+        bv, fw, bw, fac_a, fac_b, occ = [row_tiles(n) for n in ("bv", "fw", "bw", "fac_a", "fac_b", "occ")]
+        arg = [held.tile([P, S], F32, name=f"arg{t}") for t in range(PACK - 1)]
+        arg.append(held.tile([P, S], F32, name="arg_last", tag="late"))
+
+        def product(bank_cols, w, t, h):
+            nc.tensor.matmul_mx(
+                out=bank_cols,
+                lhsT=w_codes[w][:, t, :].bitcast(FP4X4),
+                lhsT_scale=w_plane[w][:, t, :],
+                rhs=xg_codes[h][:].bitcast(FP8X4),
+                rhs_scale=xg_plane[h][:],
+                start=True,
+                stop=True,
+            )
+
+        back_banks = {}
+
+        def backward(t, h):
+            if (t // 2, h) not in back_banks:
+                back_banks[t // 2, h] = psum.tile([P, 2, HALF], F32, name="bank")
+                for pair in range(2):
+                    product(back_banks[t // 2, h][:, pair, :], 0, t - t % 2 + pair, h)
+            if t == 0:
+                nc.scalar.activation(bv[t][:, HALVES[h]], back_banks[t // 2, h][:, t % 2, :], ACT.Tanh)
+            else:
+                nc.scalar.activation(bv[t][:, HALVES[h]], back_banks[t // 2, h][:, t % 2, :], ACT.Sigmoid, scale=2.0)
+
+        def forward(t):
+            bank = psum.tile([P, 2, HALF], F32, name="bank")
+            for h in range(2):
+                product(bank[:, h, :], 1, t, h)
+            nc.scalar.activation(fw[t][:], bank[:].rearrange("p h j -> p (h j)"), ACT.Tanh)
+
+        def warp(t):
+            for cols in HALVES:
+                if t == 0:
+                    gather(nc, True, bw[t][:, cols], bv[t], entries(wrp_t, cols))
+                else:
+                    nc.scalar.activation(bw[t][:, cols], bv[t][:].indirect(entries(wrp_t, cols)), ACT.Copy, bias=-1.0, scale=2.0)
+
+        def argument(t):
+            for fac, root in ((fac_a, ROOT_A), (fac_b, ROOT_B)):
+                for cols in HALVES:
+                    nc.vector.scalar_tensor_tensor(fac[t][:, cols], fw[t][:, cols], root, bw[t][:, cols], ALU.mult, ALU.add)
+            for cols in HALVES:
+                nc.vector.tensor_tensor(arg[t][:, cols], fac_a[t][:, cols], fac_b[t][:, cols], ALU.mult)
+
+        def occlusion(t):
+            for cols in HALVES:
+                nc.scalar.activation(occ[t][:, cols], arg[t][:, cols], ACT.Sigmoid, bias=-0.8, scale=2.8)
+
+        early = held.tile([P, EARLY, HALF], F32, name="early")
+        for t in (1, 0, 2, 3):
+            backward(t, 0)
+        for t in range(PACK):
+            backward(t, 1)
+            forward(t)
+            warp(t)
+            if t == PACK - 1:
+                for e in range(EARLY):
+                    gather(nc, True, early[:, e, :], fw[e], entries(wr2_t, CHUNKS[0]))
+            argument(t)
+            if t >= 2:
+                occlusion(t - 2)
+        occlusion(PACK - 2)
+        occlusion(PACK - 1)
+        late = held.tile([P, 2 * PACK * S], F32, name="late", tag="late")
+
+        out_view = out.rearrange("(m p) j -> p m j", p=P)
+        for c, cols in enumerate(CHUNKS):
+            width = cols.stop - cols.start
+            base = 2 * PACK * cols.start
+            f2_late = late[:, base : base + PACK * width].rearrange("p (t j) -> p t j", t=PACK)
+            f2 = [early[:, t, :] if c == 0 and t < EARLY else f2_late[:, t, :] for t in range(PACK)]
+            occ2 = late[:, base + PACK * width : base + 2 * PACK * width].rearrange("p (t j) -> p t j", t=PACK)
+            gap = held.tile([P, PACK, width], F32, name=f"gap_{c}")
+            part = held.tile([P, PACK, width], F32, name=f"part_{c}")
+            fix = held.tile([P, PACK, width], F32, name=f"fix_{c}")
+            for t in range(EARLY if c == 0 else 0, PACK):
+                gather(nc, False, f2[t], fw[t], entries(wr2_t, cols))
+            for t in range(PACK):
+                gather(nc, False, occ2[:, t, :], occ[t], entries(wr2_t, cols))
+            for t in range(PACK):
+                nc.vector.scalar_tensor_tensor(gap[:, t, :], fw[t][:, cols], -2.0, f2[t], ALU.mult, ALU.add)
+            for t in range(PACK):
+                nc.vector.scalar_tensor_tensor(part[:, t, :], gap[:, t, :], unit_t[:, t : t + 1], occ[t][:, cols], ALU.mult, ALU.mult)
+            for t in range(PACK):
+                nc.vector.scalar_tensor_tensor(fix[:, t, :], fw[t][:, cols], unit_t[:, t : t + 1], part[:, t, :], ALU.mult, ALU.add)
+            hid = held.tile([P, width * PACK], BF16, name=f"hid_{c}", align_bytes=64)
+            nc.vector.tensor_tensor(
+                hid[:].rearrange("p (c i t) -> p c t i", i=2, t=PACK),
+                fix[:].rearrange("p t (c i) -> p c t i", i=2),
+                occ2.rearrange("p t (c i) -> p c t i", i=2),
+                ALU.mult,
+            )
+            hid_codes = held.tile([P, width], U32, name=f"hid_codes{c}", align_bytes=64)
+            hid_plane = held.tile([P, width], U8, name=f"hid_plane{c}", align_bytes=64)
+            nc.vector.quantize_mx(out=hid_codes[:].bitcast(FP8X4), scales=hid_plane[:], in_=hid[:])
+            bank = psum.tile([P, 2, HALF], F32, name="bank")
+            for m in range(N // P):
+                nc.tensor.matmul_mx(
+                    out=bank[:, m, :width],
+                    lhsT=w3_codes[:, 2 * P * m : 2 * P * (m + 1)].bitcast(FP4X4),
+                    lhsT_scale=w3_plane[:, P * m : P * (m + 1)],
+                    rhs=hid_codes[:].bitcast(FP8X4),
+                    rhs_scale=hid_plane[:],
+                    start=True,
+                    stop=True,
+                )
+            result = held.tile([P, N // P, width], F32, name=f"result{c}")
+            nc.scalar.copy(result[:], bank[:, :, :width])
+            nc.sync.dma_start(out=out_view[:, :, cols], in_=result[:])

@@ -21,8 +21,10 @@ P = 128
 PACK = 4
 HALF = S // 2
 HALVES = [slice(0, HALF), slice(HALF, S)]
-CHUNKS = [slice(0, 256), slice(256, 384), slice(384, 512)]
-EARLY = 3
+PAIRS = [slice(0, 2), slice(2, 4)]
+ON_VECTOR = (0, 1)
+F2_ON_VECTOR = ()
+WINDOW = {True: 704, False: 528}
 ROOT_SUM = 8.0 / 2.8
 ROOT_A = ROOT_SUM / 2 + math.sqrt(ROOT_SUM * ROOT_SUM / 4 - 1)
 ROOT_B = ROOT_SUM / 2 - math.sqrt(ROOT_SUM * ROOT_SUM / 4 - 1)
@@ -32,16 +34,9 @@ def entries(offsets, cols):
     return offsets[:, cols.start // 16 : cols.stop // 16]
 
 
-def load_scale_rows(queues, plane, scales):
-    for q, queue in enumerate(queues):
+def load_scale_rows(queue, quadrants, plane, scales):
+    for q in quadrants:
         queue.dma_start(out=plane[32 * q : 32 * q + 4, :].bitcast(I32), in_=scales[0, 4 * q : 4 * q + 4, :].bitcast(I32))
-
-
-def gather(nc, on_vector, out, window, offsets):
-    if on_vector:
-        nc.vector.tensor_copy(out, window[:].indirect(offsets))
-    else:
-        nc.scalar.activation(out, window[:].indirect(offsets), ACT.Copy)
 
 
 def tile_picked_yfbflo_occ_p_kernel(
@@ -58,160 +53,186 @@ def tile_picked_yfbflo_occ_p_kernel(
         x_codes = held.tile([P, T], U32, name="x_codes")
         x_plane = held.tile([P, T], U8, name="x_plane")
         raw_codes = [held.tile([P, 2 * H], U8, name=f"raw_codes{w}", tag=f"raw{w}", align_bytes=64) for w in range(2)]
-        raw_plane = [held.tile([P, H], U8, name=f"raw_plane{w}") for w in range(2)]
-        w3_plane = held.tile([P, N], U8, name="w3_plane", align_bytes=64)
+        landing = held.tile([P, H], U8, name="landing")
+        raw_plane = [held.tile([P, H], U8, name=f"raw_plane{w}", align_bytes=64) for w in range(2)]
 
-        nc.vector.memset(x_plane[:].bitcast(I32), 0)
-        for plane in raw_plane + [w3_plane]:
-            nc.gpsimd.memset(plane[:].bitcast(I32), 0)
+        for plane in [x_plane] + raw_plane:
+            nc.vector.memset(plane[:].bitcast(I32), 0)
 
         nc.sync.dma_start(offs_t[:], offs)
         nc.scalar.dma_start(out=raw_codes[0][:].bitcast(I32), in_=w2_words[0].bitcast(I32))
         nc.sync.dma_start(wrp_t[:], wrp)
         nc.scalar.dma_start(out=raw_codes[1][:].bitcast(I32), in_=w1_words[0].bitcast(I32))
         nc.sync.dma_start(wr2_t[:], wr2)
+        load_scale_rows(nc.scalar, [3], landing, w2_scales)
         nc.scalar.dma_start(out=x_codes[:].bitcast(I32), in_=x_words[0].rearrange("p n t -> p (n t)").bitcast(I32))
-        load_scale_rows([nc.sync] * 4, x_plane, x_scales)
-        load_scale_rows([nc.sync] * 3 + [nc.gpsimd], raw_plane[0], w2_scales)
-        load_scale_rows([nc.sync] * 4, raw_plane[1], w1_scales)
-        load_scale_rows([nc.sync] * 4, w3_plane, w3_scales)
+        load_scale_rows(nc.sync, range(4), x_plane, x_scales)
+        load_scale_rows(nc.sync, range(3), raw_plane[0], w2_scales)
+        load_scale_rows(nc.sync, range(4), raw_plane[1], w1_scales)
+        nc.vector.tensor_copy(raw_plane[0][96:100, :].bitcast(I32), landing[96:100, :].bitcast(I32))
+
+        bv = [held.tile([P, WINDOW[t in ON_VECTOR]], F32, name=f"bv{t}", tag=f"bv{t}") for t in range(PACK)]
+        fw = [held.tile([P, WINDOW[t in F2_ON_VECTOR]], F32, name=f"fw{t}") for t in range(PACK)]
+        for window in bv + fw:
+            nc.gpsimd.memset(window[:, S:], 0.0)
 
         w_codes = [held.tile([P, PACK, 2 * P], U8, name=f"w_codes{w}", align_bytes=64) for w in range(2)]
         w_plane = [held.tile([P, PACK, P], U8, name=f"w_plane{w}", align_bytes=64) for w in range(2)]
-        for w in range(2):
+        xg_codes = [held.tile([P, HALF], U32, name=f"xg_codes{h}", align_bytes=64) for h in range(2)]
+        xg_plane = [held.tile([P, HALF], U8, name=f"xg_plane{h}", align_bytes=64) for h in range(2)]
+
+        def deal_codes(w):
             nc.vector.tensor_copy(
                 w_codes[w][:].rearrange("p t (m b) -> p t m b", b=2),
                 raw_codes[w][:].rearrange("p (m t b) -> p t m b", t=PACK, b=2),
             )
-        unit_t = held.tile([P, PACK], F32, name="unit_t", tag="raw0", align_bytes=64)
-        w3_codes = held.tile([P, 2 * N], U8, name="w3_codes", tag="raw1", align_bytes=64)
-        nc.sync.dma_start(out=unit_t[:], in_=unit.rearrange("(p t) o -> p (t o)", t=PACK))
-        nc.sync.dma_start(out=w3_codes[:].bitcast(I32), in_=w3_words[0].bitcast(I32))
-        xg_codes = [held.tile([P, HALF], U32, name=f"xg_codes{h}", align_bytes=64) for h in range(2)]
-        xg_plane = [held.tile([P, HALF], U8, name=f"xg_plane{h}", align_bytes=64) for h in range(2)]
 
         def deal_plane(w):
             nc.vector.tensor_copy(w_plane[w][:], raw_plane[w][:].rearrange("p (m t) -> p t m", t=PACK))
 
-        nc.vector.tensor_copy(xg_plane[0][:], x_plane[:].indirect(entries(offs_t, HALVES[0])))
+        def pick(h):
+            nc.vector.tensor_copy(xg_codes[h][:], x_codes[:].indirect(entries(offs_t, HALVES[h])))
+            nc.vector.tensor_copy(xg_plane[h][:], x_plane[:].indirect(entries(offs_t, HALVES[h])))
+
+        deal_codes(0)
+        deal_codes(1)
+        pick(0)
         deal_plane(0)
-        nc.vector.tensor_copy(xg_codes[0][:], x_codes[:].indirect(entries(offs_t, HALVES[0])))
-        nc.vector.tensor_copy(xg_plane[1][:], x_plane[:].indirect(entries(offs_t, HALVES[1])))
-        nc.vector.tensor_copy(xg_codes[1][:], x_codes[:].indirect(entries(offs_t, HALVES[1])))
+        pick(1)
         deal_plane(1)
+
+        w3_plane = raw_plane[0][:, :N]
+        load_scale_rows(nc.sync, range(4), w3_plane, w3_scales)
+        unit_t = held.tile([P, PACK], F32, name="unit_t", tag="raw0", align_bytes=64)
+        w3_codes = held.tile([P, 2 * N], U8, name="w3_codes", tag="raw1", align_bytes=64)
+        nc.sync.dma_start(out=unit_t[:], in_=unit.rearrange("(p t) o -> p (t o)", t=PACK))
+        nc.sync.dma_start(out=w3_codes[:].bitcast(I32), in_=w3_words[0].bitcast(I32))
 
         def row_tiles(name):
             return [held.tile([P, S], F32, name=f"{name}{t}") for t in range(PACK)]
 
-        bv, fw, bw, fac_a, fac_b, occ = [row_tiles(n) for n in ("bv", "fw", "bw", "fac_a", "fac_b", "occ")]
-        arg = [held.tile([P, S], F32, name=f"arg{t}") for t in range(PACK - 1)]
+        bw, fac_a, fac_b, occ, gap, part = [row_tiles(n) for n in ("bw", "fac_a", "fac_b", "occ", "gap", "part")]
+        arg = [held.tile([P, S], F32, name=f"arg{t}", tag=f"arg{t}") for t in range(PACK - 1)]
         arg.append(held.tile([P, S], F32, name="arg_last", tag="late"))
 
-        def product(bank_cols, w, t, h):
-            nc.tensor.matmul_mx(
-                out=bank_cols,
-                lhsT=w_codes[w][:, t, :].bitcast(FP4X4),
-                lhsT_scale=w_plane[w][:, t, :],
-                rhs=xg_codes[h][:].bitcast(FP8X4),
-                rhs_scale=xg_plane[h][:],
-                start=True,
-                stop=True,
-            )
-
-        back_banks = {}
-
-        def backward(t, h):
-            if (t // 2, h) not in back_banks:
-                back_banks[t // 2, h] = psum.tile([P, 2, HALF], F32, name="bank")
-                for pair in range(2):
-                    product(back_banks[t // 2, h][:, pair, :], 0, t - t % 2 + pair, h)
-            if t == 0:
-                nc.scalar.activation(bv[t][:, HALVES[h]], back_banks[t // 2, h][:, t % 2, :], ACT.Tanh)
-            else:
-                nc.scalar.activation(bv[t][:, HALVES[h]], back_banks[t // 2, h][:, t % 2, :], ACT.Sigmoid, scale=2.0)
-
-        def forward(t):
+        def products(jobs):
             bank = psum.tile([P, 2, HALF], F32, name="bank")
-            for h in range(2):
-                product(bank[:, h, :], 1, t, h)
-            nc.scalar.activation(fw[t][:], bank[:].rearrange("p h j -> p (h j)"), ACT.Tanh)
-
-        def warp(t):
-            for cols in HALVES:
-                if t == 0:
-                    gather(nc, True, bw[t][:, cols], bv[t], entries(wrp_t, cols))
-                else:
-                    nc.scalar.activation(bw[t][:, cols], bv[t][:].indirect(entries(wrp_t, cols)), ACT.Copy, bias=-1.0, scale=2.0)
-
-        def argument(t):
-            for fac, root in ((fac_a, ROOT_A), (fac_b, ROOT_B)):
-                for cols in HALVES:
-                    nc.vector.scalar_tensor_tensor(fac[t][:, cols], fw[t][:, cols], root, bw[t][:, cols], ALU.mult, ALU.add)
-            for cols in HALVES:
-                nc.vector.tensor_tensor(arg[t][:, cols], fac_a[t][:, cols], fac_b[t][:, cols], ALU.mult)
-
-        def occlusion(t):
-            for cols in HALVES:
-                nc.scalar.activation(occ[t][:, cols], arg[t][:, cols], ACT.Sigmoid, bias=-0.8, scale=2.8)
-
-        early = held.tile([P, EARLY, HALF], F32, name="early")
-        for t in (1, 0, 2, 3):
-            backward(t, 0)
-        for t in range(PACK):
-            backward(t, 1)
-            forward(t)
-            warp(t)
-            if t == PACK - 1:
-                for e in range(EARLY):
-                    gather(nc, True, early[:, e, :], fw[e], entries(wr2_t, CHUNKS[0]))
-            argument(t)
-            if t >= 2:
-                occlusion(t - 2)
-        occlusion(PACK - 2)
-        occlusion(PACK - 1)
-        late = held.tile([P, 2 * PACK * S], F32, name="late", tag="late")
-
-        out_view = out.rearrange("(m p) j -> p m j", p=P)
-        for c, cols in enumerate(CHUNKS):
-            width = cols.stop - cols.start
-            base = 2 * PACK * cols.start
-            f2_late = late[:, base : base + PACK * width].rearrange("p (t j) -> p t j", t=PACK)
-            f2 = [early[:, t, :] if c == 0 and t < EARLY else f2_late[:, t, :] for t in range(PACK)]
-            occ2 = late[:, base + PACK * width : base + 2 * PACK * width].rearrange("p (t j) -> p t j", t=PACK)
-            gap = held.tile([P, PACK, width], F32, name=f"gap_{c}")
-            part = held.tile([P, PACK, width], F32, name=f"part_{c}")
-            fix = held.tile([P, PACK, width], F32, name=f"fix_{c}")
-            for t in range(EARLY if c == 0 else 0, PACK):
-                gather(nc, False, f2[t], fw[t], entries(wr2_t, cols))
-            for t in range(PACK):
-                gather(nc, False, occ2[:, t, :], occ[t], entries(wr2_t, cols))
-            for t in range(PACK):
-                nc.vector.scalar_tensor_tensor(gap[:, t, :], fw[t][:, cols], -2.0, f2[t], ALU.mult, ALU.add)
-            for t in range(PACK):
-                nc.vector.scalar_tensor_tensor(part[:, t, :], gap[:, t, :], unit_t[:, t : t + 1], occ[t][:, cols], ALU.mult, ALU.mult)
-            for t in range(PACK):
-                nc.vector.scalar_tensor_tensor(fix[:, t, :], fw[t][:, cols], unit_t[:, t : t + 1], part[:, t, :], ALU.mult, ALU.add)
-            hid = held.tile([P, width * PACK], BF16, name=f"hid_{c}", align_bytes=64)
-            nc.vector.tensor_tensor(
-                hid[:].rearrange("p (c i t) -> p c t i", i=2, t=PACK),
-                fix[:].rearrange("p t (c i) -> p c t i", i=2),
-                occ2.rearrange("p t (c i) -> p c t i", i=2),
-                ALU.mult,
-            )
-            hid_codes = held.tile([P, width], U32, name=f"hid_codes{c}", align_bytes=64)
-            hid_plane = held.tile([P, width], U8, name=f"hid_plane{c}", align_bytes=64)
-            nc.vector.quantize_mx(out=hid_codes[:].bitcast(FP8X4), scales=hid_plane[:], in_=hid[:])
-            bank = psum.tile([P, 2, HALF], F32, name="bank")
-            for m in range(N // P):
+            for slot, (w, t, h) in enumerate(jobs):
                 nc.tensor.matmul_mx(
-                    out=bank[:, m, :width],
-                    lhsT=w3_codes[:, 2 * P * m : 2 * P * (m + 1)].bitcast(FP4X4),
-                    lhsT_scale=w3_plane[:, P * m : P * (m + 1)],
-                    rhs=hid_codes[:].bitcast(FP8X4),
-                    rhs_scale=hid_plane[:],
+                    out=bank[:, slot, :],
+                    lhsT=w_codes[w][:, t, :].bitcast(FP4X4),
+                    lhsT_scale=w_plane[w][:, t, :],
+                    rhs=xg_codes[h][:].bitcast(FP8X4),
+                    rhs_scale=xg_plane[h][:],
                     start=True,
                     stop=True,
                 )
-            result = held.tile([P, N // P, width], F32, name=f"result{c}")
-            nc.scalar.copy(result[:], bank[:, :, :width])
-            nc.sync.dma_start(out=out_view[:, :, cols], in_=result[:])
+            return bank
+
+        def whole_row(w, t):
+            return products([(w, t, 0), (w, t, 1)])[:].rearrange("p h j -> p (h j)")
+
+        def backward(t, cols, sums):
+            if t in ON_VECTOR:
+                nc.scalar.activation(bv[t][:, cols], sums, ACT.Tanh)
+            else:
+                nc.scalar.activation(bv[t][:, cols], sums, ACT.Sigmoid, scale=2.0)
+
+        def forward(t):
+            nc.scalar.activation(fw[t][:, :S], whole_row(1, t), ACT.Tanh)
+
+        def warp(t):
+            if t in ON_VECTOR:
+                nc.vector.tensor_copy(bw[t][:], bv[t][:].indirect(wrp_t[:]))
+            else:
+                nc.scalar.activation(bw[t][:], bv[t][:].indirect(wrp_t[:]), ACT.Copy, bias=-1.0, scale=2.0)
+
+        def factors(t):
+            for fac, root in ((fac_a, ROOT_A), (fac_b, ROOT_B)):
+                nc.vector.scalar_tensor_tensor(fac[t][:], fw[t][:, :S], root, bw[t][:], ALU.mult, ALU.add)
+
+        def occlusion(t):
+            nc.vector.tensor_tensor(arg[t][:], fac_a[t][:], fac_b[t][:], ALU.mult)
+            nc.scalar.activation(occ[t][:], arg[t][:], ACT.Sigmoid, bias=-0.8, scale=2.8)
+
+        fix = held.tile([P, PACK, S], F32, name="fix")
+        f2 = {}
+
+        def neighbour(t, reuse):
+            f2[t] = held.tile([P, S], F32, name=f"f2_{t}", tag=reuse)
+            if t in F2_ON_VECTOR:
+                nc.vector.tensor_copy(f2[t][:], fw[t][:].indirect(wr2_t[:]))
+            else:
+                nc.scalar.activation(f2[t][:], fw[t][:].indirect(wr2_t[:]), ACT.Copy)
+
+        def repair(t):
+            gain = unit_t[:, t : t + 1]
+            nc.vector.scalar_tensor_tensor(gap[t][:], fw[t][:, :S], -2.0, f2[t][:], ALU.mult, ALU.add)
+            nc.vector.scalar_tensor_tensor(part[t][:], gap[t][:], gain, occ[t][:], ALU.mult, ALU.mult)
+            nc.vector.scalar_tensor_tensor(fix[:, t, :], fw[t][:, :S], gain, part[t][:], ALU.mult, ALU.add)
+
+        backward(2, HALVES[0], products([(0, 2, 0)])[:, 0, :])
+        backward(0, HALVES[0], products([(0, 0, 0)])[:, 0, :])
+        second = products([(0, 0, 1), (0, 2, 1)])
+        backward(0, HALVES[1], second[:, 0, :])
+        warp(0)
+        backward(1, slice(0, S), whole_row(0, 1))
+        warp(1)
+        forward(0)
+        forward(1)
+        backward(2, HALVES[1], second[:, 1, :])
+        backward(3, slice(0, S), whole_row(0, 3))
+        factors(0)
+        forward(2)
+        warp(2)
+        factors(1)
+        occlusion(0)
+        forward(3)
+        warp(3)
+        occlusion(1)
+        factors(2)
+        factors(3)
+        occlusion(2)
+        occlusion(3)
+        for t, reuse in enumerate(("bv3", "arg0", "arg1", "arg2")):
+            neighbour(t, reuse)
+        for t in range(PACK):
+            repair(t)
+
+        late = held.tile([P, 2, PACK, HALF], F32, name="late", tag="late")
+        occ2 = [late[:, 0], late[:, 1]]
+
+        for c, cols in enumerate(HALVES):
+            for t in range(PACK):
+                nc.scalar.activation(occ2[c][:, t, :], occ[t][:].indirect(entries(wr2_t, cols)), ACT.Copy)
+            width = HALF // (c + 1)
+            for s in range(c + 1):
+                sub = slice(s * width, (s + 1) * width)
+                hid = held.tile([P, width * PACK], BF16, name=f"hid_{c}{s}", align_bytes=64)
+                nc.vector.tensor_tensor(
+                    hid[:].rearrange("p (c i t) -> p c t i", i=2, t=PACK),
+                    fix[:, :, cols.start + sub.start : cols.start + sub.stop].rearrange("p t (c i) -> p c t i", i=2),
+                    occ2[c][:, :, sub].rearrange("p t (c i) -> p c t i", i=2),
+                    ALU.mult,
+                )
+                hid_codes = held.tile([P, width], U32, name=f"hid_codes{c}{s}", align_bytes=64)
+                hid_plane = held.tile([P, width], U8, name=f"hid_plane{c}{s}", align_bytes=64)
+                nc.vector.quantize_mx(out=hid_codes[:].bitcast(FP8X4), scales=hid_plane[:], in_=hid[:])
+                for m in range(N // P):
+                    bank = psum.tile([P, 2, HALF], F32, name="bank")
+                    nc.tensor.matmul_mx(
+                        out=bank[:, 0, :width],
+                        lhsT=w3_codes[:, 2 * P * m : 2 * P * (m + 1)].bitcast(FP4X4),
+                        lhsT_scale=w3_plane[:, P * m : P * (m + 1)],
+                        rhs=hid_codes[:].bitcast(FP8X4),
+                        rhs_scale=hid_plane[:],
+                        start=True,
+                        stop=True,
+                    )
+                    result = held.tile([P, width], F32, name=f"result{c}{s}{m}")
+                    if (c, s, m) in ((0, 0, 1), (1, 1, 1)):
+                        nc.vector.tensor_copy(result[:], bank[:, 0, :width])
+                    else:
+                        nc.scalar.copy(result[:], bank[:, 0, :width])
+                    queue = nc.scalar if m == 0 and c == 1 else nc.sync
+                    queue.dma_start(out=out[P * m : P * (m + 1), cols.start + sub.start : cols.start + sub.stop], in_=result[:])

@@ -165,11 +165,13 @@ def tile_picked_yfbflo_occ_p_kernel(
             else:
                 nc.scalar.activation(f2[t][:], fw[t][:].indirect(wr2_t[:]), ACT.Copy)
 
-        def repair(t):
-            gain = unit_t[:, t : t + 1]
-            nc.vector.scalar_tensor_tensor(gap[t][:], fw[t][:, :S], -2.0, f2[t][:], ALU.mult, ALU.add)
-            nc.vector.scalar_tensor_tensor(part[t][:], gap[t][:], gain, occ[t][:], ALU.mult, ALU.mult)
-            nc.vector.scalar_tensor_tensor(fix[:, t, :], fw[t][:, :S], gain, part[t][:], ALU.mult, ALU.add)
+        def repair(tiles):
+            for t in tiles:
+                nc.vector.scalar_tensor_tensor(gap[t][:], fw[t][:, :S], -2.0, f2[t][:], ALU.mult, ALU.add)
+            for t in tiles:
+                nc.vector.scalar_tensor_tensor(part[t][:], gap[t][:], unit_t[:, t : t + 1], occ[t][:], ALU.mult, ALU.mult)
+            for t in tiles:
+                nc.vector.scalar_tensor_tensor(fix[:, t, :], fw[t][:, :S], unit_t[:, t : t + 1], part[t][:], ALU.mult, ALU.add)
 
         backward(2, HALVES[0], products([(0, 2, 0)])[:, 0, :])
         backward(0, HALVES[0], products([(0, 0, 0)])[:, 0, :])
@@ -196,25 +198,33 @@ def tile_picked_yfbflo_occ_p_kernel(
         occlusion(3)
         for t, reuse in enumerate(("bv3", "arg0", "arg1", "arg2")):
             neighbour(t, reuse)
-        for t in range(PACK):
-            repair(t)
+        repair((0, 1))
+        repair((2, 3))
 
         late = held.tile([P, 2, PACK, HALF], F32, name="late", tag="late")
-        occ2 = [late[:, 0], late[:, 1]]
+        quarters = late[:, 1].rearrange("p t j -> p (t j)").rearrange("p (s t j) -> p s t j", s=2, t=PACK)
+        occ2 = [[late[:, 0, :, :P], late[:, 0, :, P:]], [quarters[:, 0], quarters[:, 1]]]
 
         for c, cols in enumerate(HALVES):
-            for t in range(PACK):
-                nc.scalar.activation(occ2[c][:, t, :], occ[t][:].indirect(entries(wr2_t, cols)), ACT.Copy)
-            width = HALF // (c + 1)
-            for s in range(c + 1):
+            step = HALF // (c + 1)
+            for j in range(0, HALF, step):
+                for t in range(PACK):
+                    picked = entries(wr2_t, slice(cols.start + j, cols.start + j + step))
+                    nc.scalar.activation(late[:, 0, t, :] if c == 0 else occ2[c][j // step][:, t, :], occ[t][:].indirect(picked), ACT.Copy)
+            width = HALF // 2
+            hids = []
+            for s in range(2):
                 sub = slice(s * width, (s + 1) * width)
                 hid = held.tile([P, width * PACK], BF16, name=f"hid_{c}{s}", align_bytes=64)
                 nc.vector.tensor_tensor(
                     hid[:].rearrange("p (c i t) -> p c t i", i=2, t=PACK),
                     fix[:, :, cols.start + sub.start : cols.start + sub.stop].rearrange("p t (c i) -> p c t i", i=2),
-                    occ2[c][:, :, sub].rearrange("p t (c i) -> p c t i", i=2),
+                    occ2[c][s].rearrange("p t (c i) -> p c t i", i=2),
                     ALU.mult,
                 )
+                hids.append(hid)
+            for s, hid in enumerate(hids):
+                sub = slice(s * width, (s + 1) * width)
                 hid_codes = held.tile([P, width], U32, name=f"hid_codes{c}{s}", align_bytes=64)
                 hid_plane = held.tile([P, width], U8, name=f"hid_plane{c}{s}", align_bytes=64)
                 nc.vector.quantize_mx(out=hid_codes[:].bitcast(FP8X4), scales=hid_plane[:], in_=hid[:])
@@ -230,7 +240,7 @@ def tile_picked_yfbflo_occ_p_kernel(
                         stop=True,
                     )
                     result = held.tile([P, width], F32, name=f"result{c}{s}{m}")
-                    if (c, s, m) in ((0, 0, 1), (1, 1, 1)):
+                    if (c, s, m) in ((1, 1, 1),):
                         nc.vector.tensor_copy(result[:], bank[:, 0, :width])
                     else:
                         nc.scalar.copy(result[:], bank[:, 0, :width])

@@ -56,7 +56,7 @@ def tile_picked_yfbflo_occ_p_kernel(
         landing = held.tile([P, H], U8, name="landing")
         raw_plane = [held.tile([P, H], U8, name=f"raw_plane{w}", align_bytes=64) for w in range(2)]
 
-        for plane in [x_plane] + raw_plane:
+        for plane in (raw_plane[0], x_plane, raw_plane[1]):
             nc.vector.memset(plane[:].bitcast(I32), 0)
 
         nc.sync.dma_start(offs_t[:], offs)
@@ -66,8 +66,8 @@ def tile_picked_yfbflo_occ_p_kernel(
         nc.sync.dma_start(wr2_t[:], wr2)
         load_scale_rows(nc.scalar, [3], landing, w2_scales)
         nc.scalar.dma_start(out=x_codes[:].bitcast(I32), in_=x_words[0].rearrange("p n t -> p (n t)").bitcast(I32))
-        load_scale_rows(nc.sync, range(4), x_plane, x_scales)
         load_scale_rows(nc.sync, range(3), raw_plane[0], w2_scales)
+        load_scale_rows(nc.sync, range(4), x_plane, x_scales)
         load_scale_rows(nc.sync, range(4), raw_plane[1], w1_scales)
         nc.vector.tensor_copy(raw_plane[0][96:100, :].bitcast(I32), landing[96:100, :].bitcast(I32))
 
@@ -96,8 +96,8 @@ def tile_picked_yfbflo_occ_p_kernel(
 
         deal_codes(0)
         deal_codes(1)
-        pick(0)
         deal_plane(0)
+        pick(0)
         pick(1)
         deal_plane(1)
 

import math
from contextlib import ExitStack

import concourse.mybir as mybir

K, T, S, H, N = 512, 2048, 512, 512, 256
FLOPS = 2 * K * H * S * 2 + 2 * H * N * S

F32 = mybir.dt.float32
BF16 = mybir.dt.bfloat16
I32 = mybir.dt.int32
U32 = mybir.dt.uint32
U16 = mybir.dt.uint16
U8 = mybir.dt.uint8
FP8X4 = mybir.dt.float8_e4m3fn_x4
FP4X4 = mybir.dt.float4_e2m1fn_x4
ALU = mybir.AluOpType
ACT = mybir.ActivationFunctionType

P = 128
PACK = 4
HALF = S // 2
HALVES = [slice(0, HALF), slice(HALF, S)]
PAIRS = [slice(0, 2), slice(2, 4)]
ON_VECTOR = (0, 1)
F2_ON_VECTOR = ()
WINDOW = {True: 704, False: 528}
ROOT_SUM = 8.0 / 2.8
ROOT_A = ROOT_SUM / 2 + math.sqrt(ROOT_SUM * ROOT_SUM / 4 - 1)
ROOT_B = ROOT_SUM / 2 - math.sqrt(ROOT_SUM * ROOT_SUM / 4 - 1)


def entries(offsets, cols):
    return offsets[:, cols.start // 16 : cols.stop // 16]


def load_scale_rows(queue, quadrants, plane, scales):
    for q in quadrants:
        queue.dma_start(out=plane[32 * q : 32 * q + 4, :].bitcast(I32), in_=scales[0, 4 * q : 4 * q + 4, :].bitcast(I32))


def tile_picked_yfbflo_occ_p_kernel(
    tc, x_words, x_scales, w1_words, w1_scales, w2_words, w2_scales, unit, w3_words, w3_scales, offs, wrp, wr2, out
):
    nc = tc.nc
    with ExitStack() as ctx:
        held = ctx.enter_context(tc.tile_pool(name="held", bufs=1))
        psum = ctx.enter_context(tc.psum_pool(name="psum", bufs=8))

        offs_t = held.tile([P, S // 16], U16, name="offs_t")
        wrp_t = held.tile([P, S // 16], U16, name="wrp_t")
        wr2_t = held.tile([P, S // 16], U16, name="wr2_t")
        x_codes = held.tile([P, T], U32, name="x_codes")
        x_plane = held.tile([P, T], U8, name="x_plane")
        raw_codes = [held.tile([P, 2 * H], U8, name=f"raw_codes{w}", tag=f"raw{w}", align_bytes=64) for w in range(2)]
        landing = held.tile([P, H], U8, name="landing")
        raw_plane = [held.tile([P, H], U8, name=f"raw_plane{w}", align_bytes=64) for w in range(2)]

        for plane in (raw_plane[0], x_plane, raw_plane[1]):
            nc.vector.memset(plane[:].bitcast(I32), 0)

        nc.sync.dma_start(offs_t[:], offs)
        nc.scalar.dma_start(out=raw_codes[0][:].bitcast(I32), in_=w2_words[0].bitcast(I32))
        nc.sync.dma_start(wrp_t[:], wrp)
        nc.scalar.dma_start(out=raw_codes[1][:].bitcast(I32), in_=w1_words[0].bitcast(I32))
        nc.sync.dma_start(wr2_t[:], wr2)
        load_scale_rows(nc.scalar, [3], landing, w2_scales)
        nc.scalar.dma_start(out=x_codes[:].bitcast(I32), in_=x_words[0].rearrange("p n t -> p (n t)").bitcast(I32))
        load_scale_rows(nc.sync, range(3), raw_plane[0], w2_scales)
        load_scale_rows(nc.sync, range(4), x_plane, x_scales)
        load_scale_rows(nc.sync, range(4), raw_plane[1], w1_scales)
        nc.vector.tensor_copy(raw_plane[0][96:100, :].bitcast(I32), landing[96:100, :].bitcast(I32))

        bv = [held.tile([P, WINDOW[t in ON_VECTOR]], F32, name=f"bv{t}", tag=f"bv{t}") for t in range(PACK)]
        fw = [held.tile([P, WINDOW[t in F2_ON_VECTOR]], F32, name=f"fw{t}") for t in range(PACK)]
        for window in bv + fw:
            nc.gpsimd.memset(window[:, S:], 0.0)

        w_codes = [held.tile([P, PACK, 2 * P], U8, name=f"w_codes{w}", align_bytes=64) for w in range(2)]
        w_plane = [held.tile([P, PACK, P], U8, name=f"w_plane{w}", align_bytes=64) for w in range(2)]
        xg_codes = [held.tile([P, HALF], U32, name=f"xg_codes{h}", align_bytes=64) for h in range(2)]
        xg_plane = [held.tile([P, HALF], U8, name=f"xg_plane{h}", align_bytes=64) for h in range(2)]

        def deal_codes(w):
            nc.vector.tensor_copy(
                w_codes[w][:].rearrange("p t (m b) -> p t m b", b=2),
                raw_codes[w][:].rearrange("p (m t b) -> p t m b", t=PACK, b=2),
            )

        def deal_plane(w):
            nc.vector.tensor_copy(w_plane[w][:], raw_plane[w][:].rearrange("p (m t) -> p t m", t=PACK))

        def pick(h):
            nc.vector.tensor_copy(xg_codes[h][:], x_codes[:].indirect(entries(offs_t, HALVES[h])))
            nc.vector.tensor_copy(xg_plane[h][:], x_plane[:].indirect(entries(offs_t, HALVES[h])))

        deal_codes(0)
        deal_codes(1)
        deal_plane(0)
        pick(0)
        pick(1)
        deal_plane(1)

        w3_plane = raw_plane[0][:, :N]
        load_scale_rows(nc.sync, range(4), w3_plane, w3_scales)
        unit_t = held.tile([P, PACK], F32, name="unit_t", tag="raw0", align_bytes=64)
        w3_codes = held.tile([P, 2 * N], U8, name="w3_codes", tag="raw1", align_bytes=64)
        nc.sync.dma_start(out=unit_t[:], in_=unit.rearrange("(p t) o -> p (t o)", t=PACK))
        nc.sync.dma_start(out=w3_codes[:].bitcast(I32), in_=w3_words[0].bitcast(I32))

        def row_tiles(name):
            return [held.tile([P, S], F32, name=f"{name}{t}") for t in range(PACK)]

        bw, fac_a, fac_b, occ, gap, part = [row_tiles(n) for n in ("bw", "fac_a", "fac_b", "occ", "gap", "part")]
        arg = [held.tile([P, S], F32, name=f"arg{t}", tag=f"arg{t}") for t in range(PACK - 1)]
        arg.append(held.tile([P, S], F32, name="arg_last", tag="late"))

        def products(jobs):
            bank = psum.tile([P, 2, HALF], F32, name="bank")
            for slot, (w, t, h) in enumerate(jobs):
                nc.tensor.matmul_mx(
                    out=bank[:, slot, :],
                    lhsT=w_codes[w][:, t, :].bitcast(FP4X4),
                    lhsT_scale=w_plane[w][:, t, :],
                    rhs=xg_codes[h][:].bitcast(FP8X4),
                    rhs_scale=xg_plane[h][:],
                    start=True,
                    stop=True,
                )
            return bank

        def whole_row(w, t):
            return products([(w, t, 0), (w, t, 1)])[:].rearrange("p h j -> p (h j)")

        def backward(t, cols, sums):
            if t in ON_VECTOR:
                nc.scalar.activation(bv[t][:, cols], sums, ACT.Tanh)
            else:
                nc.scalar.activation(bv[t][:, cols], sums, ACT.Sigmoid, scale=2.0)

        def forward(t):
            nc.scalar.activation(fw[t][:, :S], whole_row(1, t), ACT.Tanh)

        def warp(t):
            if t in ON_VECTOR:
                nc.vector.tensor_copy(bw[t][:], bv[t][:].indirect(wrp_t[:]))
            else:
                nc.scalar.activation(bw[t][:], bv[t][:].indirect(wrp_t[:]), ACT.Copy, bias=-1.0, scale=2.0)

        def factors(t):
            for fac, root in ((fac_a, ROOT_A), (fac_b, ROOT_B)):
                nc.vector.scalar_tensor_tensor(fac[t][:], fw[t][:, :S], root, bw[t][:], ALU.mult, ALU.add)

        def occlusion(t):
            nc.vector.tensor_tensor(arg[t][:], fac_a[t][:], fac_b[t][:], ALU.mult)
            nc.scalar.activation(occ[t][:], arg[t][:], ACT.Sigmoid, bias=-0.8, scale=2.8)

        fix = held.tile([P, PACK, S], F32, name="fix")
        f2 = {}

        def neighbour(t, reuse):
            f2[t] = held.tile([P, S], F32, name=f"f2_{t}", tag=reuse)
            if t in F2_ON_VECTOR:
                nc.vector.tensor_copy(f2[t][:], fw[t][:].indirect(wr2_t[:]))
            else:
                nc.scalar.activation(f2[t][:], fw[t][:].indirect(wr2_t[:]), ACT.Copy)

        def repair(tiles):
            for t in tiles:
                nc.vector.scalar_tensor_tensor(gap[t][:], fw[t][:, :S], -2.0, f2[t][:], ALU.mult, ALU.add)
            for t in tiles:
                nc.vector.scalar_tensor_tensor(part[t][:], gap[t][:], unit_t[:, t : t + 1], occ[t][:], ALU.mult, ALU.mult)
            for t in tiles:
                nc.vector.scalar_tensor_tensor(fix[:, t, :], fw[t][:, :S], unit_t[:, t : t + 1], part[t][:], ALU.mult, ALU.add)

        backward(2, HALVES[0], products([(0, 2, 0)])[:, 0, :])
        backward(0, HALVES[0], products([(0, 0, 0)])[:, 0, :])
        second = products([(0, 0, 1), (0, 2, 1)])
        backward(0, HALVES[1], second[:, 0, :])
        warp(0)
        backward(1, slice(0, S), whole_row(0, 1))
        warp(1)
        forward(0)
        forward(1)
        backward(2, HALVES[1], second[:, 1, :])
        backward(3, slice(0, S), whole_row(0, 3))
        factors(0)
        forward(2)
        warp(2)
        factors(1)
        occlusion(0)
        forward(3)
        warp(3)
        occlusion(1)
        factors(2)
        factors(3)
        occlusion(2)
        occlusion(3)
        for t, reuse in enumerate(("bv3", "arg0", "arg1", "arg2")):
            neighbour(t, reuse)
        repair((0, 1))
        repair((2, 3))

        late = held.tile([P, 2, PACK, HALF], F32, name="late", tag="late")
        quarters = late[:, 1].rearrange("p t j -> p (t j)").rearrange("p (s t j) -> p s t j", s=2, t=PACK)
        occ2 = [[late[:, 0, :, :P], late[:, 0, :, P:]], [quarters[:, 0], quarters[:, 1]]]

        for c, cols in enumerate(HALVES):
            step = HALF // (c + 1)
            for j in range(0, HALF, step):
                for t in range(PACK):
                    picked = entries(wr2_t, slice(cols.start + j, cols.start + j + step))
                    nc.scalar.activation(late[:, 0, t, :] if c == 0 else occ2[c][j // step][:, t, :], occ[t][:].indirect(picked), ACT.Copy)
            width = HALF // 2
            hids = []
            for s in range(2):
                sub = slice(s * width, (s + 1) * width)
                hid = held.tile([P, width * PACK], BF16, name=f"hid_{c}{s}", align_bytes=64)
                nc.vector.tensor_tensor(
                    hid[:].rearrange("p (c i t) -> p c t i", i=2, t=PACK),
                    fix[:, :, cols.start + sub.start : cols.start + sub.stop].rearrange("p t (c i) -> p c t i", i=2),
                    occ2[c][s].rearrange("p t (c i) -> p c t i", i=2),
                    ALU.mult,
                )
                hids.append(hid)
            for s, hid in enumerate(hids):
                sub = slice(s * width, (s + 1) * width)
                hid_codes = held.tile([P, width], U32, name=f"hid_codes{c}{s}", align_bytes=64)
                hid_plane = held.tile([P, width], U8, name=f"hid_plane{c}{s}", align_bytes=64)
                nc.vector.quantize_mx(out=hid_codes[:].bitcast(FP8X4), scales=hid_plane[:], in_=hid[:])
                for m in range(N // P):
                    bank = psum.tile([P, 2, HALF], F32, name="bank")
                    nc.tensor.matmul_mx(
                        out=bank[:, 0, :width],
                        lhsT=w3_codes[:, 2 * P * m : 2 * P * (m + 1)].bitcast(FP4X4),
                        lhsT_scale=w3_plane[:, P * m : P * (m + 1)],
                        rhs=hid_codes[:].bitcast(FP8X4),
                        rhs_scale=hid_plane[:],
                        start=True,
                        stop=True,
                    )
                    result = held.tile([P, width], F32, name=f"result{c}{s}{m}")
                    if (c, s, m) in ((1, 1, 1),):
                        nc.vector.tensor_copy(result[:], bank[:, 0, :width])
                    else:
                        nc.scalar.copy(result[:], bank[:, 0, :width])
                    queue = nc.scalar if m == 0 and c == 1 else nc.sync
                    queue.dma_start(out=out[P * m : P * (m + 1), cols.start + sub.start : cols.start + sub.stop], in_=result[:])
